import numpy as np
import ml_dtypes


def mxq(x, axis, fmt="e4m3"):
    dtype, down = {"e4m3": (ml_dtypes.float8_e4m3fn, 7), "e5m2": (ml_dtypes.float8_e5m2, 14)}[fmt]
    v = np.moveaxis(np.asarray(x, np.float32).astype(ml_dtypes.bfloat16).astype(np.float64), axis, -1)
    blocks = v.reshape(v.shape[:-1] + (-1, 32))
    amax = np.abs(blocks).max(-1, keepdims=True)
    byte = np.maximum(np.where(amax > 0, np.frexp(amax)[1] - 1 + 127, 0) - down, 1)
    scale = np.exp2(byte - 127.0)
    codes = (blocks / scale).astype(np.float32).astype(dtype).astype(np.float64)
    return np.moveaxis((codes * scale).reshape(v.shape), -1, axis)


WIDE = False


def mx_kscale(k):
    if not WIDE:
        return np.ones(k)
    levels = np.array([10, -10, 5, -5, 0])
    if k % 512:
        return np.exp2(np.random.permutation(np.resize(levels, k // 32))).repeat(32)
    a = np.empty((k // 512, 16))
    for p in range(k // 512):
        a[p, :8] = np.random.permutation(np.resize(levels, 8))
        for g in range(8):
            far = levels[np.abs(levels - a[p, g]) >= 10]
            a[p, g + 8] = far[np.random.randint(len(far))]
    return np.exp2(a.ravel()).repeat(32)


def f64(x):
    return np.asarray(x).astype(np.float64)


def striped(idx):
    return np.tile(idx.reshape(-1, 16).T, (8, 1)).astype(np.uint16)


def unstriped(offs):
    return offs[:16].T.reshape(-1).astype(np.int64)


def pack_weight(w):
    k, n = w.shape
    w = f64(np.asarray(w, np.float32).astype(ml_dtypes.bfloat16)).reshape(k // 32, 32, n)
    amax = np.abs(w).max(1)
    byte = np.clip(np.where(amax > 0, np.frexp(amax)[1] - 1 + 127 - 7, 1), 1, 254)
    scaled = (w * np.exp2(127.0 - byte)[:, None, :]).reshape(k, n).astype(np.float32)
    words = np.ascontiguousarray(scaled.reshape(k // 512, 128, 4, n).transpose(0, 1, 3, 2)).astype(ml_dtypes.float8_e4m3fn).view(np.uint8)
    return words, np.ascontiguousarray(byte.astype(np.uint8).reshape(k // 512, 16, n))


def unpack_weight(words, scales):
    g, p, n, _ = words.shape
    vals = np.ascontiguousarray(words).view(ml_dtypes.float8_e4m3fn).astype(np.float64) * np.repeat(np.exp2(scales.astype(np.float64) - 127.0), 8, axis=1)[..., None]
    return vals.transpose(0, 1, 3, 2).reshape(g * 512, n)


K, T, S, N = 1024, 2048, 512, 128


def setup_inputs():
    n = np.random.standard_normal
    s = mx_kscale(K)[:, None]
    packed_xT = pack_weight(n((K, T)) * s)
    return {
        "x_words": packed_xT[0],
        "x_scales": packed_xT[1],
        "w1": (n((K, N)) / np.sqrt(K) / s).astype(np.float32),
        "w2": (n((K, N)) / np.sqrt(K) / s).astype(np.float32),
        "tap0": (0.4 * n((N, 1))).astype(np.float32),
        "tap1": (0.4 * n((N, 1))).astype(np.float32),
        "tap2": (0.4 * n((N, 1))).astype(np.float32),
        "tap3": (0.4 * n((N, 1))).astype(np.float32),
        "offs": striped(np.random.permutation(T)[:S]),
    }


def reference(x_words, x_scales, w1, w2, tap0, tap1, tap2, tap3, offs):
    xq = unpack_weight(x_words, x_scales)[:, unstriped(offs)]
    mic = mxq(f64(w2), 0, "e4m3").T @ xq
    far = mxq(f64(w1), 0, "e4m3").T @ xq
    echo = f64(tap0) * far + f64(tap1) * (np.pad(far, ((0, 0), (1, 0)))[:, :S]) + f64(tap2) * (np.pad(far, ((0, 0), (2, 0)))[:, :S]) + f64(tap3) * (np.pad(far, ((0, 0), (3, 0)))[:, :S])
    err = mic - echo
    pw = (far) ** 2 + (np.pad(far, ((0, 0), (1, 0)))[:, :S]) ** 2 + (np.pad(far, ((0, 0), (2, 0)))[:, :S]) ** 2 + (np.pad(far, ((0, 0), (3, 0)))[:, :S]) ** 2 + 0.5
    st = err / pw
    return (((err) ** 2) / (0.5 * ((np.pad(err, ((0, 0), (1, 0)))[:, :S]) ** 2) + 0.5 * ((mic) ** 2) + 0.4)) * np.tanh(2.0 * st)

@@ -1,0 +1,178 @@
+import concourse.mybir as mybir
+from contextlib import ExitStack
+
+K, T, S, N = 1024, 2048, 512, 128
+FLOPS = 2 * 2 * K * N * S
+F32 = mybir.dt.float32
+BF16 = mybir.dt.bfloat16
+U32 = mybir.dt.uint32
+I32 = mybir.dt.int32
+U16 = mybir.dt.uint16
+U8 = mybir.dt.uint8
+FP8X4 = mybir.dt.float8_e4m3fn_x4
+ALU = mybir.AluOpType
+ACT = mybir.ActivationFunctionType
+P = 128
+H = S // 2
+
+
+def tile_picked_ynlms_dtd_p_kernel(tc, x_words, x_scales, w1, w2, tap0, tap1, tap2, tap3, offs, out):
+    nc = tc.nc
+    eng = {"s": nc.sync, "a": nc.scalar, "g": nc.gpsimd}
+    with ExitStack() as ctx:
+        keep = ctx.enter_context(tc.tile_pool(name="keep", bufs=1))
+        stage = ctx.enter_context(tc.tile_pool(name="stage", bufs=1))
+        psum = ctx.enter_context(tc.psum_pool(name="psum", bufs=1))
+
+        offsets = keep.tile([P, S // 16], U16, name="offsets")
+        nc.sync.dma_start(offsets[:], offs)
+
+        xs = keep.tile([P, T], U8, name="xs", align_bytes=64)
+        nc.gpsimd.memset(xs[:].bitcast(I32), 0)
+        one = stage.tile([P, 32], F32, name="one", offset=24576)
+        nc.vector.memset(one[:], 1.0)
+        warm = keep.tile([P, 32], F32, name="warm")
+        nc.scalar.activation(warm[:], one[:], ACT.Abs_reciprocal_sqrt)
+
+        acc = keep.tile([P, S], F32, name="acc")
+        sq = keep.tile([P, 8 + S], F32, name="sq")
+        e2 = keep.tile([P, 8 + S], F32, name="e2")
+        nc.vector.memset(acc[:, 0:3], 0.0)
+        nc.vector.memset(sq[:, 0:8], 0.0)
+        nc.vector.memset(e2[:, 0:8], 0.0)
+
+        def load_w(w, g, name):
+            raw = stage.tile([P, 4, N], F32, name=name, offset=4096 + 2048 * g)
+            nc.sync.dma_start(raw[:], w[512 * g : 512 * (g + 1), :].rearrange("(p j) m -> p j m", j=4))
+            return raw[:]
+
+        def load_x(g):
+            xw = stage.tile([P, T], U32, name="xw%d" % g, offset=16384 - 16320 * g)
+            nc.sync.dma_start(xw[:].bitcast(I32), x_words[g].rearrange("p n t -> p (n t)").bitcast(I32))
+            return xw
+
+        def load_scales():
+            for q in range(4):
+                eng["a"].dma_start(xs[32 * q : 32 * q + 8, :].bitcast(I32), x_scales[:, 4 * q : 4 * q + 4, :].bitcast(I32))
+
+        taps = []
+        def load_taps():
+            for s, tp in reversed(list(enumerate((tap0, tap1, tap2, tap3)))):
+                t = stage.tile([P, 1], F32, name="tap%d" % s, offset=8192 + 128 + 32 * s)
+                eng["s"].dma_start(t[:], tp)
+                taps.insert(0, t)
+
+        raw = {}
+        xw = {}
+        for item in ["w1","w2","x0","sc"]:
+            if item == "sc":
+                load_scales()
+            elif item == "w1":
+                both = stage.tile([P, 2, 4, N], F32, name="raww1", offset=8192)
+                nc.sync.dma_start(both[:], w1.rearrange("(g p j) m -> p g j m", g=2, j=4))
+                raw["w10"], raw["w11"] = both[:, 0], both[:, 1]
+            elif item == "w2":
+                both2 = stage.tile([P, 2, 4, N], F32, name="raww2", offset=12288)
+                nc.sync.dma_start(both2[:], w2.rearrange("(g p j) m -> p g j m", g=2, j=4))
+                raw["w20"], raw["w21"] = both2[:, 0], both2[:, 1]
+            elif item[0] == "x":
+                xw[int(item[1])] = load_x(int(item[1]))
+            else:
+                raw[item] = load_w(w1 if item[1] == "1" else w2, int(item[2]), "raw" + item)
+
+        wq = {}
+        def quant(item, e):
+            grouped = keep.tile([P, N, 4], BF16, name="grp" + item, align_bytes=64)
+            dst = grouped[:].rearrange("p (c i) t -> p c t i", i=4) if True else grouped[:]
+            src = raw[item].rearrange("p t (c i) -> p c t i", i=4) if True else raw[item].rearrange("p j m -> p m j")
+            if e == "a":
+                nc.scalar.copy(dst, src)
+            elif e == "v":
+                nc.vector.tensor_copy(dst, src)
+            else:
+                nc.gpsimd.tensor_scalar(dst, src, 1.0, 0.0, ALU.mult, ALU.add)
+            codes = keep.tile([P, N], U32, name="wc" + item, align_bytes=64)
+            scales = keep.tile([P, N], U8, name="ws" + item, align_bytes=64)
+            nc.vector.quantize_mx(out=codes[:].bitcast(FP8X4), scales=scales[:], in_=grouped[:].rearrange("p m j -> p (m j)"))
+            wq[item] = (codes, scales)
+
+        quant("w10", "v")
+        quant("w11", "v")
+        quant("w20", "v")
+        quant("w21", "v")
+        xw[1] = load_x(1)
+        load_taps()
+        gs = keep.tile([P, S], U8, name="gs", align_bytes=64)
+        nc.vector.tensor_copy(gs[:], xs[:].indirect(offsets[:]))
+        g0 = keep.tile([P, S], U32, name="g0", align_bytes=64)
+        nc.vector.tensor_copy(g0[:], xw[0][:].indirect(offsets[:]))
+        far = [psum.tile([P, 512], F32, name="far%d" % h) for h in range(2)]
+        mic = [psum.tile([P, 512], F32, name="mic%d" % h) for h in range(2)]
+
+        def mm(dst, item, g, h, rhs):
+            codes, scales = wq[item]
+            nc.tensor.matmul_mx(out=dst[h][:, 0:H], lhsT=codes[:].bitcast(FP8X4), lhsT_scale=scales[:], rhs=rhs.bitcast(FP8X4),
+                                rhs_scale=gs[4 * g : P, H * h : H * (h + 1)], start=(g == 0), stop=(g == 1))
+
+        for h in range(2):
+            mm(far, "w10", 0, h, g0[:, H * h : H * (h + 1)])
+            mm(mic, "w20", 0, h, g0[:, H * h : H * (h + 1)])
+        g1 = []
+        for h in range(2):
+            t = keep.tile([P, H], U32, name="g1%d" % h, align_bytes=64)
+            nc.vector.tensor_copy(t[:], xw[1][:].indirect(offsets[:, 16 * h : 16 * (h + 1)]))
+            g1.append(t)
+            mm(far, "w11", 1, h, t[:])
+            mm(mic, "w21", 1, h, t[:])
+
+        pe = nc.gpsimd
+        q2 = keep.tile([P, 8 + S], F32, name="q2")
+        pw = keep.tile([P, S], F32, name="pw")
+        rp = keep.tile([P, S], F32, name="rp")
+        m2 = keep.tile([P, S], F32, name="m2")
+        ne = keep.tile([P, S], F32, name="ne")
+        den = keep.tile([P, S], F32, name="den")
+        rd = keep.tile([P, S], F32, name="rd")
+        u = keep.tile([P, S], F32, name="u")
+        gg = keep.tile([P, S], F32, name="gg")
+        res = keep.tile([P, S], F32, name="res")
+
+        def cols(h, lo=0, hi=0):
+            return slice(H * h + lo, H * (h + 1) + hi)
+
+        for h in range(2):
+            c0 = H * h
+            n3 = H if h == 0 else H - 3
+            nc.scalar.activation(acc[:, c0 + 3 : c0 + 3 + n3], far[h][:, 0:n3], ACT.Copy, scale=taps[3][:])
+            nc.scalar.activation(sq[:, cols(h, 8, 8)], far[h][:, 0:H], ACT.Square)
+        for h in range(2):
+            lo = -2 if h == 0 else 0
+            pe.tensor_tensor(q2[:, cols(h, 8 + lo, 8)], sq[:, cols(h, 8 + lo, 8)], sq[:, cols(h, 7 + lo, 7)], ALU.add)
+            pe.tensor_tensor(pw[:, cols(h)], q2[:, cols(h, 8, 8)], q2[:, cols(h, 6, 6)], ALU.add)
+        for s in (2, 1, 0):
+            for h in range(2):
+                c0 = H * h
+                ns = H if h == 0 else H - s
+                nc.vector.scalar_tensor_tensor(acc[:, c0 + s : c0 + s + ns], far[h][:, 0:ns], taps[s][:], acc[:, c0 + s : c0 + s + ns], ALU.mult, ALU.add)
+        for h in range(2):
+            nc.scalar.activation(m2[:, cols(h)], mic[h][:, 0:H], ACT.Square)
+            nc.vector.tensor_tensor(ne[:, cols(h)], acc[:, cols(h)], mic[h][:, 0:H], ALU.subtract)
+        for h in range(2):
+            nc.scalar.activation(e2[:, cols(h, 8, 8)], ne[:, cols(h)], ACT.Square)
+            nc.scalar.activation(rp[:, cols(h)], pw[:, cols(h)], ACT.Abs_reciprocal_sqrt, bias=0.5)
+        for h in range(2):
+            nc.vector.tensor_tensor(den[:, cols(h)], e2[:, cols(h, 7, 7)], m2[:, cols(h)], ALU.add)
+        for h in range(2):
+            nc.scalar.activation(rd[:, cols(h)], den[:, cols(h)], ACT.Abs_reciprocal_sqrt, bias=0.4, scale=0.5)
+        for h in range(2):
+            nc.vector.tensor_tensor(u[:, cols(h)], ne[:, cols(h)], rp[:, cols(h)], ALU.mult)
+        for h in range(2):
+            nc.vector.tensor_tensor(u[:, cols(h)], u[:, cols(h)], rp[:, cols(h)], ALU.mult)
+        for h in range(2):
+            nc.vector.tensor_tensor(gg[:, cols(h)], e2[:, cols(h, 8, 8)], rd[:, cols(h)], ALU.mult)
+        for h in range(2):
+            nc.vector.tensor_tensor(gg[:, cols(h)], gg[:, cols(h)], rd[:, cols(h)], ALU.mult)
+        for h in range(2):
+            nc.scalar.activation(den[:, cols(1 - h)], u[:, cols(h)], ACT.Tanh, scale=-2.0)
+            nc.vector.tensor_tensor(res[:, cols(h)], gg[:, cols(h)], den[:, cols(1 - h)], ALU.mult)
+            eng["sa"[h]].dma_start(out[:, cols(h)], res[:, cols(h)])

@@ -1,4 +1,5 @@
 import concourse.mybir as mybir
+from concourse.masks import make_identity
 from contextlib import ExitStack
 
 K, T, S, N = 1024, 2048, 512, 128
@@ -27,8 +28,10 @@ def tile_picked_ynlms_dtd_p_kernel(tc, x_words, x_scales, w1, w2, tap0, tap1, ta
         offsets = keep.tile([P, S // 16], U16, name="offsets")
         nc.sync.dma_start(offsets[:], offs)
 
+        ident = keep.tile([P, P], F32, name="ident")
+        make_identity(nc, ident[:])
         xs = keep.tile([P, T], U8, name="xs", align_bytes=64)
-        nc.gpsimd.memset(xs[:].bitcast(I32), 0)
+        nc.vector.memset(xs[:].bitcast(I32), 0)
         one = stage.tile([P, 32], F32, name="one", offset=24576)
         nc.vector.memset(one[:], 1.0)
         warm = keep.tile([P, 32], F32, name="warm")
@@ -42,12 +45,12 @@ def tile_picked_ynlms_dtd_p_kernel(tc, x_words, x_scales, w1, w2, tap0, tap1, ta
         nc.vector.memset(e2[:, 0:8], 0.0)
 
         def load_w(w, g, name):
-            raw = stage.tile([P, 4, N], F32, name=name, offset=4096 + 2048 * g)
+            raw = stage.tile([P, 4, N], F32, name=name, offset={"raww10": 8192, "raww11": 12288, "raww20": 8192 + 2048 - 64, "raww21": 12288}[name])
             nc.sync.dma_start(raw[:], w[512 * g : 512 * (g + 1), :].rearrange("(p j) m -> p j m", j=4))
             return raw[:]
 
         def load_x(g):
-            xw = stage.tile([P, T], U32, name="xw%d" % g, offset=16384 - 16320 * g)
+            xw = stage.tile([P, T], U32, name="xw%d" % g, offset=(16384, 64)[g])
             nc.sync.dma_start(xw[:].bitcast(I32), x_words[g].rearrange("p n t -> p (n t)").bitcast(I32))
             return xw
 
@@ -58,23 +61,21 @@ def tile_picked_ynlms_dtd_p_kernel(tc, x_words, x_scales, w1, w2, tap0, tap1, ta
         taps = []
         def load_taps():
             for s, tp in reversed(list(enumerate((tap0, tap1, tap2, tap3)))):
-                t = stage.tile([P, 1], F32, name="tap%d" % s, offset=8192 + 128 + 32 * s)
-                eng["s"].dma_start(t[:], tp)
+                t = keep.tile([P, 1], F32, name="tap%d" % s)
+                eng["g"].dma_start(t[:], tp)
                 taps.insert(0, t)
 
         raw = {}
         xw = {}
-        for item in ["w1","w2","x0","sc"]:
+        for item in ["tp","w10","w11","x0","sc"]:
             if item == "sc":
                 load_scales()
+            elif item == "tp":
+                load_taps()
             elif item == "w1":
-                both = stage.tile([P, 2, 4, N], F32, name="raww1", offset=8192)
+                both = stage.tile([P, 2, 4, N], F32, name="raww1", offset=0)
                 nc.sync.dma_start(both[:], w1.rearrange("(g p j) m -> p g j m", g=2, j=4))
                 raw["w10"], raw["w11"] = both[:, 0], both[:, 1]
-            elif item == "w2":
-                both2 = stage.tile([P, 2, 4, N], F32, name="raww2", offset=12288)
-                nc.sync.dma_start(both2[:], w2.rearrange("(g p j) m -> p g j m", g=2, j=4))
-                raw["w20"], raw["w21"] = both2[:, 0], both2[:, 1]
             elif item[0] == "x":
                 xw[int(item[1])] = load_x(int(item[1]))
             else:
@@ -98,10 +99,9 @@ def tile_picked_ynlms_dtd_p_kernel(tc, x_words, x_scales, w1, w2, tap0, tap1, ta
 
         quant("w10", "v")
         quant("w11", "v")
-        quant("w20", "v")
-        quant("w21", "v")
         xw[1] = load_x(1)
-        load_taps()
+        raw["w20"] = load_w(w2, 0, "raww20")
+        raw["w21"] = load_w(w2, 1, "raww21")
         gs = keep.tile([P, S], U8, name="gs", align_bytes=64)
         nc.vector.tensor_copy(gs[:], xs[:].indirect(offsets[:]))
         g0 = keep.tile([P, S], U32, name="g0", align_bytes=64)
@@ -116,18 +116,19 @@ def tile_picked_ynlms_dtd_p_kernel(tc, x_words, x_scales, w1, w2, tap0, tap1, ta
 
         for h in range(2):
             mm(far, "w10", 0, h, g0[:, H * h : H * (h + 1)])
-            mm(mic, "w20", 0, h, g0[:, H * h : H * (h + 1)])
         g1 = []
         for h in range(2):
             t = keep.tile([P, H], U32, name="g1%d" % h, align_bytes=64)
             nc.vector.tensor_copy(t[:], xw[1][:].indirect(offsets[:, 16 * h : 16 * (h + 1)]))
             g1.append(t)
             mm(far, "w11", 1, h, t[:])
-            mm(mic, "w21", 1, h, t[:])
+        quant("w20", "a")
+        quant("w21", "v")
+        for h in range(2):
+            mm(mic, "w20", 0, h, g0[:, H * h : H * (h + 1)])
+        for h in range(2):
+            mm(mic, "w21", 1, h, g1[h][:])
 
-        pe = nc.gpsimd
-        q2 = keep.tile([P, 8 + S], F32, name="q2")
-        pw = keep.tile([P, S], F32, name="pw")
         rp = keep.tile([P, S], F32, name="rp")
         m2 = keep.tile([P, S], F32, name="m2")
         ne = keep.tile([P, S], F32, name="ne")
@@ -143,12 +144,15 @@ def tile_picked_ynlms_dtd_p_kernel(tc, x_words, x_scales, w1, w2, tap0, tap1, ta
         for h in range(2):
             c0 = H * h
             n3 = H if h == 0 else H - 3
-            nc.scalar.activation(acc[:, c0 + 3 : c0 + 3 + n3], far[h][:, 0:n3], ACT.Copy, scale=taps[3][:])
             nc.scalar.activation(sq[:, cols(h, 8, 8)], far[h][:, 0:H], ACT.Square)
+            nc.scalar.activation(acc[:, c0 + 3 : c0 + 3 + n3], far[h][:, 0:n3], ACT.Copy, scale=taps[3][:])
+        pwt = [psum.tile([P, 512], F32, name="pwt%d" % h) for h in range(2)]
+        rpb = [psum.tile([P, 512], F32, name="rpb%d" % h) for h in range(2)]
         for h in range(2):
-            lo = -2 if h == 0 else 0
-            pe.tensor_tensor(q2[:, cols(h, 8 + lo, 8)], sq[:, cols(h, 8 + lo, 8)], sq[:, cols(h, 7 + lo, 7)], ALU.add)
-            pe.tensor_tensor(pw[:, cols(h)], q2[:, cols(h, 8, 8)], q2[:, cols(h, 6, 6)], ALU.add)
+            for t in range(2):
+                c0 = 8 + H * h + P * t
+                for s in range(4):
+                    nc.tensor.matmul(pwt[h][:, P * t : P * (t + 1)], sq[:, c0 - s : c0 - s + P], ident[:], start=(s == 0), stop=(s == 3), is_transpose=True)
         for s in (2, 1, 0):
             for h in range(2):
                 c0 = H * h
@@ -159,15 +163,20 @@ def tile_picked_ynlms_dtd_p_kernel(tc, x_words, x_scales, w1, w2, tap0, tap1, ta
             nc.vector.tensor_tensor(ne[:, cols(h)], acc[:, cols(h)], mic[h][:, 0:H], ALU.subtract)
         for h in range(2):
             nc.scalar.activation(e2[:, cols(h, 8, 8)], ne[:, cols(h)], ACT.Square)
-            nc.scalar.activation(rp[:, cols(h)], pw[:, cols(h)], ACT.Abs_reciprocal_sqrt, bias=0.5)
+        for h in range(2):
+            nc.scalar.activation(rp[:, cols(h)], pwt[h][:, 0:H], ACT.Abs_reciprocal_sqrt, bias=0.5)
+            for t in range(2):
+                nc.tensor.transpose(rpb[h][:, P * t : P * (t + 1)], rp[:, H * h + P * t : H * h + P * (t + 1)], ident[:])
         for h in range(2):
             nc.vector.tensor_tensor(den[:, cols(h)], e2[:, cols(h, 7, 7)], m2[:, cols(h)], ALU.add)
         for h in range(2):
             nc.scalar.activation(rd[:, cols(h)], den[:, cols(h)], ACT.Abs_reciprocal_sqrt, bias=0.4, scale=0.5)
+        warm2 = keep.tile([P, 8], F32, name="warm2")
+        nc.scalar.activation(warm2[:], rd[:, S - 8 : S], ACT.Tanh)
         for h in range(2):
-            nc.vector.tensor_tensor(u[:, cols(h)], ne[:, cols(h)], rp[:, cols(h)], ALU.mult)
+            nc.vector.tensor_tensor(u[:, cols(h)], ne[:, cols(h)], rpb[h][:, 0:H], ALU.mult)
         for h in range(2):
-            nc.vector.tensor_tensor(u[:, cols(h)], u[:, cols(h)], rp[:, cols(h)], ALU.mult)
+            nc.vector.tensor_tensor(u[:, cols(h)], u[:, cols(h)], rpb[h][:, 0:H], ALU.mult)
         for h in range(2):
             nc.vector.tensor_tensor(gg[:, cols(h)], e2[:, cols(h, 8, 8)], rd[:, cols(h)], ALU.mult)
         for h in range(2):

@@ -33,16 +33,15 @@ def tile_picked_ynlms_dtd_p_kernel(tc, x_words, x_scales, w1, w2, tap0, tap1, ta
         xs = keep.tile([P, T], U8, name="xs", align_bytes=64)
         nc.vector.memset(xs[:].bitcast(I32), 0)
         one = stage.tile([P, 32], F32, name="one", offset=24576)
-        nc.vector.memset(one[:], 1.0)
-        warm = keep.tile([P, 32], F32, name="warm")
-        nc.scalar.activation(warm[:], one[:], ACT.Abs_reciprocal_sqrt)
 
         acc = keep.tile([P, S], F32, name="acc")
         sq = keep.tile([P, 8 + S], F32, name="sq")
         e2 = keep.tile([P, 8 + S], F32, name="e2")
         nc.vector.memset(acc[:, 0:3], 0.0)
-        nc.vector.memset(sq[:, 0:8], 0.0)
-        nc.vector.memset(e2[:, 0:8], 0.0)
+        za = stage.tile([P, 16], F32, name="za", offset=16352)
+        nc.vector.memset(za[:], 0.0)
+        nc.vector.tensor_copy(sq[:, 0:8], za[:, 0:8])
+        nc.vector.tensor_copy(e2[:, 0:8], za[:, 8:16])
 
         def load_w(w, g, name):
             raw = stage.tile([P, 4, N], F32, name=name, offset={"raww10": 8192, "raww11": 12288, "raww20": 8192 + 2048 - 64, "raww21": 12288}[name])
@@ -56,18 +55,27 @@ def tile_picked_ynlms_dtd_p_kernel(tc, x_words, x_scales, w1, w2, tap0, tap1, ta
 
         def load_scales():
             for q in range(4):
-                eng["a"].dma_start(xs[32 * q : 32 * q + 8, :].bitcast(I32), x_scales[:, 4 * q : 4 * q + 4, :].bitcast(I32))
+                eng["aaaa"[q]].dma_start(xs[32 * q : 32 * q + 8, :].bitcast(I32), x_scales[:, 4 * q : 4 * q + 4, :].bitcast(I32))
 
         taps = []
         def load_taps():
-            for s, tp in reversed(list(enumerate((tap0, tap1, tap2, tap3)))):
-                t = keep.tile([P, 1], F32, name="tap%d" % s)
-                eng["g"].dma_start(t[:], tp)
-                taps.insert(0, t)
+            rows = stage.tile([P, P], F32, name="taprows", offset=15872)
+            nc.vector.memset(rows[:], 0.0)
+            nc.vector.tensor_scalar(one[:], rows[:, 0:32], 0.0, 1.0, ALU.mult, ALU.add)
+            for s, tp in enumerate((tap0, tap1, tap2, tap3)):
+                nc.scalar.dma_start(rows[s : s + 1, :], tp.rearrange("p o -> o p"))
+            warm = keep.tile([P, 32], F32, name="warm")
+            nc.scalar.activation(warm[:], one[:], ACT.Abs_reciprocal_sqrt)
+            tps = psum.tile([P, 512], F32, name="tps", tag="rpb0")
+            nc.tensor.transpose(tps[:, 0:P], rows[:], ident[:])
+            tapt = keep.tile([P, 4], F32, name="tapt")
+            nc.scalar.copy(tapt[:], tps[:, 0:4])
+            for s in range(4):
+                taps.append(tapt[:, s : s + 1])
 
         raw = {}
         xw = {}
-        for item in ["tp","w10","w11","x0","sc"]:
+        for item in ["w10","w11","x0","sc","tp"]:
             if item == "sc":
                 load_scales()
             elif item == "tp":
@@ -145,9 +153,9 @@ def tile_picked_ynlms_dtd_p_kernel(tc, x_words, x_scales, w1, w2, tap0, tap1, ta
             c0 = H * h
             n3 = H if h == 0 else H - 3
             nc.scalar.activation(sq[:, cols(h, 8, 8)], far[h][:, 0:H], ACT.Square)
-            nc.scalar.activation(acc[:, c0 + 3 : c0 + 3 + n3], far[h][:, 0:n3], ACT.Copy, scale=taps[3][:])
+            nc.scalar.activation(acc[:, c0 + 3 : c0 + 3 + n3], far[h][:, 0:n3], ACT.Copy, scale=taps[3])
         pwt = [psum.tile([P, 512], F32, name="pwt%d" % h) for h in range(2)]
-        rpb = [psum.tile([P, 512], F32, name="rpb%d" % h) for h in range(2)]
+        rpb = [psum.tile([P, 512], F32, name="rpb%d" % h, tag="rpb%d" % h) for h in range(2)]
         for h in range(2):
             for t in range(2):
                 c0 = 8 + H * h + P * t
@@ -157,7 +165,7 @@ def tile_picked_ynlms_dtd_p_kernel(tc, x_words, x_scales, w1, w2, tap0, tap1, ta
             for h in range(2):
                 c0 = H * h
                 ns = H if h == 0 else H - s
-                nc.vector.scalar_tensor_tensor(acc[:, c0 + s : c0 + s + ns], far[h][:, 0:ns], taps[s][:], acc[:, c0 + s : c0 + s + ns], ALU.mult, ALU.add)
+                nc.vector.scalar_tensor_tensor(acc[:, c0 + s : c0 + s + ns], far[h][:, 0:ns], taps[s], acc[:, c0 + s : c0 + s + ns], ALU.mult, ALU.add)
         for h in range(2):
             nc.scalar.activation(m2[:, cols(h)], mic[h][:, 0:H], ACT.Square)
             nc.vector.tensor_tensor(ne[:, cols(h)], acc[:, cols(h)], mic[h][:, 0:H], ALU.subtract)

@@ -1,9 +1,10 @@
-import concourse.mybir as mybir
-from concourse.masks import make_identity
 from contextlib import ExitStack
+
+import concourse.mybir as mybir
 
 K, T, S, N = 1024, 2048, 512, 128
 FLOPS = 2 * 2 * K * N * S
+
 F32 = mybir.dt.float32
 BF16 = mybir.dt.bfloat16
 U32 = mybir.dt.uint32
@@ -13,183 +14,192 @@ U8 = mybir.dt.uint8
 FP8X4 = mybir.dt.float8_e4m3fn_x4
 ALU = mybir.AluOpType
 ACT = mybir.ActivationFunctionType
+
 P = 128
-H = S // 2
+PACK = 4
+K_PASS = P * PACK
+HALF = S // 2
+BANK = 512
+PAD = 8
+
+WORDS_BYTES = T * 4
+RAW_BYTES = PACK * N * 4
+AT_W1 = (WORDS_BYTES, WORDS_BYTES + 2 * RAW_BYTES)
+AT_X1 = 64
+AT_W2 = (AT_W1[0] + RAW_BYTES - 64, AT_W1[1])
+AT_X0 = 2 * WORDS_BYTES
+AT_ZERO = AT_X0 - PAD * 4
+AT_PAIRS = AT_X0 + WORDS_BYTES
 
 
-def tile_picked_ynlms_dtd_p_kernel(tc, x_words, x_scales, w1, w2, tap0, tap1, tap2, tap3, offs, out):
+def tile_picked_ynlms_dtd_p_kernel(
+    tc, x_words, x_scales, w1, w2, tap0, tap1, tap2, tap3, offs, out
+):
     nc = tc.nc
-    eng = {"s": nc.sync, "a": nc.scalar, "g": nc.gpsimd}
+
+    def half(h, shift=0):
+        return slice(HALF * h + shift, HALF * (h + 1) + shift)
+
     with ExitStack() as ctx:
         keep = ctx.enter_context(tc.tile_pool(name="keep", bufs=1))
-        stage = ctx.enter_context(tc.tile_pool(name="stage", bufs=1))
+        shared = ctx.enter_context(tc.tile_pool(name="shared", bufs=1))
         psum = ctx.enter_context(tc.psum_pool(name="psum", bufs=1))
 
         offsets = keep.tile([P, S // 16], U16, name="offsets")
         nc.sync.dma_start(offsets[:], offs)
 
-        ident = keep.tile([P, P], F32, name="ident")
-        make_identity(nc, ident[:])
-        xs = keep.tile([P, T], U8, name="xs", align_bytes=64)
-        nc.vector.memset(xs[:].bitcast(I32), 0)
-        one = stage.tile([P, 32], F32, name="one", offset=24576)
+        zero = shared.tile([P, 2 * PAD], F32, name="zero", offset=AT_ZERO)
+        nc.vector.memset(zero[:], 0.0)
+        scale_rows = keep.tile([P, T], U8, name="scale_rows", align_bytes=64)
+        nc.vector.memset(scale_rows[:].bitcast(I32), 0)
+        far_sq = keep.tile([P, PAD + S], F32, name="far_sq")
+        err_sq = keep.tile([P, PAD + S], F32, name="err_sq")
+        nc.vector.tensor_copy(far_sq[:, 0:PAD], zero[:, 0:PAD])
+        nc.vector.tensor_copy(err_sq[:, 0:PAD], zero[:, PAD : 2 * PAD])
+        echo = keep.tile([P, S], F32, name="echo")
+        nc.vector.memset(echo[:, 0:3], 0.0)
+        ones = keep.tile([P, PAD], F32, name="ones")
+        nc.vector.memset(ones[:], 1.0)
 
-        acc = keep.tile([P, S], F32, name="acc")
-        sq = keep.tile([P, 8 + S], F32, name="sq")
-        e2 = keep.tile([P, 8 + S], F32, name="e2")
-        nc.vector.memset(acc[:, 0:3], 0.0)
-        za = stage.tile([P, 16], F32, name="za", offset=16352)
-        nc.vector.memset(za[:], 0.0)
-        nc.vector.tensor_copy(sq[:, 0:8], za[:, 0:8])
-        nc.vector.tensor_copy(e2[:, 0:8], za[:, 8:16])
+        taps = {}
+        for s, tap in ((3, tap3), (2, tap2), (1, tap1), (0, tap0)):
+            taps[s] = keep.tile([P, 1], F32, name="tap%d" % s)
+            nc.gpsimd.dma_start(taps[s][:], tap)
 
-        def load_w(w, g, name):
-            raw = stage.tile([P, 4, N], F32, name=name, offset={"raww10": 8192, "raww11": 12288, "raww20": 8192 + 2048 - 64, "raww21": 12288}[name])
-            nc.sync.dma_start(raw[:], w[512 * g : 512 * (g + 1), :].rearrange("(p j) m -> p j m", j=4))
-            return raw[:]
+        def load_weights(w, g, name, at):
+            raw = shared.tile([P, PACK, N], F32, name=name, offset=at)
+            nc.sync.dma_start(raw[:], w[K_PASS * g : K_PASS * (g + 1), :].rearrange("(p t) m -> p t m", t=PACK))
+            return raw
 
-        def load_x(g):
-            xw = stage.tile([P, T], U32, name="xw%d" % g, offset=(16384, 64)[g])
-            nc.sync.dma_start(xw[:].bitcast(I32), x_words[g].rearrange("p n t -> p (n t)").bitcast(I32))
-            return xw
+        def load_words(g, at):
+            words = shared.tile([P, T], U32, name="words%d" % g, offset=at)
+            nc.sync.dma_start(words[:].bitcast(I32), x_words[g].rearrange("p n t -> p (n t)").bitcast(I32))
+            return words
 
-        def load_scales():
-            for q in range(4):
-                eng["aaaa"[q]].dma_start(xs[32 * q : 32 * q + 8, :].bitcast(I32), x_scales[:, 4 * q : 4 * q + 4, :].bitcast(I32))
+        def quantise(raw, name, copy, grouped):
+            copy(
+                grouped[:].rearrange("p (c i) t -> p c t i", i=4),
+                raw[:].rearrange("p t (c i) -> p c t i", i=4),
+            )
+            codes = keep.tile([P, N], U32, name="codes_" + name, align_bytes=64)
+            scales = keep.tile([P, N], U8, name="scales_" + name, align_bytes=64)
+            nc.vector.quantize_mx(
+                out=codes[:].bitcast(FP8X4), scales=scales[:], in_=grouped[:].rearrange("p m t -> p (m t)")
+            )
+            return codes, scales
 
-        taps = []
-        def load_taps():
-            rows = stage.tile([P, P], F32, name="taprows", offset=15872)
-            nc.vector.memset(rows[:], 0.0)
-            nc.vector.tensor_scalar(one[:], rows[:, 0:32], 0.0, 1.0, ALU.mult, ALU.add)
-            for s, tp in enumerate((tap0, tap1, tap2, tap3)):
-                nc.scalar.dma_start(rows[s : s + 1, :], tp.rearrange("p o -> o p"))
-            warm = keep.tile([P, 32], F32, name="warm")
-            nc.scalar.activation(warm[:], one[:], ACT.Abs_reciprocal_sqrt)
-            tps = psum.tile([P, 512], F32, name="tps", tag="rpb0")
-            nc.tensor.transpose(tps[:, 0:P], rows[:], ident[:])
-            tapt = keep.tile([P, 4], F32, name="tapt")
-            nc.scalar.copy(tapt[:], tps[:, 0:4])
-            for s in range(4):
-                taps.append(tapt[:, s : s + 1])
+        def grouped_tile(name):
+            return keep.tile([P, N, PACK], BF16, name="grouped_" + name, align_bytes=64)
 
-        raw = {}
-        xw = {}
-        for item in ["w10","w11","x0","sc","tp"]:
-            if item == "sc":
-                load_scales()
-            elif item == "tp":
-                load_taps()
-            elif item == "w1":
-                both = stage.tile([P, 2, 4, N], F32, name="raww1", offset=0)
-                nc.sync.dma_start(both[:], w1.rearrange("(g p j) m -> p g j m", g=2, j=4))
-                raw["w10"], raw["w11"] = both[:, 0], both[:, 1]
-            elif item[0] == "x":
-                xw[int(item[1])] = load_x(int(item[1]))
-            else:
-                raw[item] = load_w(w1 if item[1] == "1" else w2, int(item[2]), "raw" + item)
+        raw_w1 = [load_weights(w1, g, "raw_w1_%d" % g, AT_W1[g]) for g in range(2)]
+        words0 = load_words(0, AT_X0)
+        for r in range(4):
+            for g in range(2):
+                nc.scalar.dma_start(
+                    scale_rows[4 * g + r : P : 32, :].bitcast(I32), x_scales[g, r:16:4, :].bitcast(I32)
+                )
+        preload_rsqrt = keep.tile([P, PAD], F32, name="preload_rsqrt")
+        nc.scalar.activation(preload_rsqrt[:], ones[:], ACT.Abs_reciprocal_sqrt)
 
-        wq = {}
-        def quant(item, e):
-            grouped = keep.tile([P, N, 4], BF16, name="grp" + item, align_bytes=64)
-            dst = grouped[:].rearrange("p (c i) t -> p c t i", i=4) if True else grouped[:]
-            src = raw[item].rearrange("p t (c i) -> p c t i", i=4) if True else raw[item].rearrange("p j m -> p m j")
-            if e == "a":
-                nc.scalar.copy(dst, src)
-            elif e == "v":
-                nc.vector.tensor_copy(dst, src)
-            else:
-                nc.gpsimd.tensor_scalar(dst, src, 1.0, 0.0, ALU.mult, ALU.add)
-            codes = keep.tile([P, N], U32, name="wc" + item, align_bytes=64)
-            scales = keep.tile([P, N], U8, name="ws" + item, align_bytes=64)
-            nc.vector.quantize_mx(out=codes[:].bitcast(FP8X4), scales=scales[:], in_=grouped[:].rearrange("p m j -> p (m j)"))
-            wq[item] = (codes, scales)
+        q_w1 = [
+            quantise(raw_w1[g], "w1_%d" % g, nc.vector.tensor_copy, grouped_tile("w1_%d" % g)) for g in range(2)
+        ]
+        words1 = load_words(1, AT_X1)
+        raw_w2 = [load_weights(w2, g, "raw_w2_%d" % g, AT_W2[g]) for g in range(2)]
 
-        quant("w10", "v")
-        quant("w11", "v")
-        xw[1] = load_x(1)
-        raw["w20"] = load_w(w2, 0, "raww20")
-        raw["w21"] = load_w(w2, 1, "raww21")
-        gs = keep.tile([P, S], U8, name="gs", align_bytes=64)
-        nc.vector.tensor_copy(gs[:], xs[:].indirect(offsets[:]))
-        g0 = keep.tile([P, S], U32, name="g0", align_bytes=64)
-        nc.vector.tensor_copy(g0[:], xw[0][:].indirect(offsets[:]))
-        far = [psum.tile([P, 512], F32, name="far%d" % h) for h in range(2)]
-        mic = [psum.tile([P, 512], F32, name="mic%d" % h) for h in range(2)]
+        picked_scales = keep.tile([P, S], U8, name="picked_scales", align_bytes=64)
+        nc.vector.tensor_copy(picked_scales[:], scale_rows[:].indirect(offsets[:]))
+        picked0 = keep.tile([P, S], U32, name="picked0", align_bytes=64)
+        nc.vector.tensor_copy(picked0[:], words0[:].indirect(offsets[:]))
 
-        def mm(dst, item, g, h, rhs):
-            codes, scales = wq[item]
-            nc.tensor.matmul_mx(out=dst[h][:, 0:H], lhsT=codes[:].bitcast(FP8X4), lhsT_scale=scales[:], rhs=rhs.bitcast(FP8X4),
-                                rhs_scale=gs[4 * g : P, H * h : H * (h + 1)], start=(g == 0), stop=(g == 1))
+        far = [psum.tile([P, BANK], F32, name="far%d" % h) for h in range(2)]
+        mic = [psum.tile([P, BANK], F32, name="mic%d" % h) for h in range(2)]
+
+        def product_pass(bank, weights, g, h, picked):
+            codes, scales = weights
+            nc.tensor.matmul_mx(
+                out=bank[:, 0:HALF],
+                lhsT=codes[:].bitcast(FP8X4),
+                lhsT_scale=scales[:],
+                rhs=picked.bitcast(FP8X4),
+                rhs_scale=picked_scales[4 * g : P, half(h)],
+                start=(g == 0),
+                stop=(g == 1),
+            )
 
         for h in range(2):
-            mm(far, "w10", 0, h, g0[:, H * h : H * (h + 1)])
-        g1 = []
+            product_pass(far[h], q_w1[0], 0, h, picked0[:, half(h)])
+        picked1 = []
         for h in range(2):
-            t = keep.tile([P, H], U32, name="g1%d" % h, align_bytes=64)
-            nc.vector.tensor_copy(t[:], xw[1][:].indirect(offsets[:, 16 * h : 16 * (h + 1)]))
-            g1.append(t)
-            mm(far, "w11", 1, h, t[:])
-        quant("w20", "a")
-        quant("w21", "v")
+            picked1.append(keep.tile([P, HALF], U32, name="picked1_%d" % h, align_bytes=64))
+            nc.vector.tensor_copy(picked1[h][:], words1[:].indirect(offsets[:, 16 * h : 16 * (h + 1)]))
+            product_pass(far[h], q_w1[1], 1, h, picked1[h][:])
+        last_grouped = shared.tile([P, N, PACK], BF16, name="grouped_w2_1", offset=AT_PAIRS, align_bytes=64)
+        q_w2 = [
+            quantise(raw_w2[0], "w2_0", nc.scalar.copy, grouped_tile("w2_0")),
+            quantise(raw_w2[1], "w2_1", nc.vector.tensor_copy, last_grouped),
+        ]
         for h in range(2):
-            mm(mic, "w20", 0, h, g0[:, H * h : H * (h + 1)])
+            product_pass(mic[h], q_w2[0], 0, h, picked0[:, half(h)])
         for h in range(2):
-            mm(mic, "w21", 1, h, g1[h][:])
-
-        rp = keep.tile([P, S], F32, name="rp")
-        m2 = keep.tile([P, S], F32, name="m2")
-        ne = keep.tile([P, S], F32, name="ne")
-        den = keep.tile([P, S], F32, name="den")
-        rd = keep.tile([P, S], F32, name="rd")
-        u = keep.tile([P, S], F32, name="u")
-        gg = keep.tile([P, S], F32, name="gg")
-        res = keep.tile([P, S], F32, name="res")
-
-        def cols(h, lo=0, hi=0):
-            return slice(H * h + lo, H * (h + 1) + hi)
+            product_pass(mic[h], q_w2[1], 1, h, picked1[h][:])
 
         for h in range(2):
-            c0 = H * h
-            n3 = H if h == 0 else H - 3
-            nc.scalar.activation(sq[:, cols(h, 8, 8)], far[h][:, 0:H], ACT.Square)
-            nc.scalar.activation(acc[:, c0 + 3 : c0 + 3 + n3], far[h][:, 0:n3], ACT.Copy, scale=taps[3])
-        pwt = [psum.tile([P, 512], F32, name="pwt%d" % h) for h in range(2)]
-        rpb = [psum.tile([P, 512], F32, name="rpb%d" % h, tag="rpb%d" % h) for h in range(2)]
+            n = HALF - 3 * h
+            nc.scalar.activation(far_sq[:, half(h, PAD)], far[h][:, 0:HALF], ACT.Square)
+            nc.scalar.activation(
+                echo[:, HALF * h + 3 : HALF * h + 3 + n], far[h][:, 0:n], ACT.Copy, scale=taps[3][:]
+            )
+
+        pairs = shared.tile([P, PAD + S], F32, name="pairs", offset=AT_PAIRS)
+        power = keep.tile([P, S], F32, name="power")
         for h in range(2):
-            for t in range(2):
-                c0 = 8 + H * h + P * t
-                for s in range(4):
-                    nc.tensor.matmul(pwt[h][:, P * t : P * (t + 1)], sq[:, c0 - s : c0 - s + P], ident[:], start=(s == 0), stop=(s == 3), is_transpose=True)
+            lo = HALF * h + PAD - (2 if h == 0 else 0)
+            hi = HALF * (h + 1) + PAD
+            nc.gpsimd.tensor_tensor(pairs[:, lo:hi], far_sq[:, lo:hi], far_sq[:, lo - 1 : hi - 1], ALU.add)
+            nc.gpsimd.tensor_tensor(power[:, half(h)], pairs[:, half(h, PAD)], pairs[:, half(h, PAD - 2)], ALU.add)
+
         for s in (2, 1, 0):
             for h in range(2):
-                c0 = H * h
-                ns = H if h == 0 else H - s
-                nc.vector.scalar_tensor_tensor(acc[:, c0 + s : c0 + s + ns], far[h][:, 0:ns], taps[s], acc[:, c0 + s : c0 + s + ns], ALU.mult, ALU.add)
+                n = HALF - s * h
+                target = echo[:, HALF * h + s : HALF * h + s + n]
+                nc.vector.scalar_tensor_tensor(target, far[h][:, 0:n], taps[s][:], target, ALU.mult, ALU.add)
+
+        mic_sq = keep.tile([P, S], F32, name="mic_sq")
+        neg_err = keep.tile([P, S], F32, name="neg_err")
         for h in range(2):
-            nc.scalar.activation(m2[:, cols(h)], mic[h][:, 0:H], ACT.Square)
-            nc.vector.tensor_tensor(ne[:, cols(h)], acc[:, cols(h)], mic[h][:, 0:H], ALU.subtract)
+            nc.scalar.activation(mic_sq[:, half(h)], mic[h][:, 0:HALF], ACT.Square)
+            nc.vector.tensor_tensor(neg_err[:, half(h)], echo[:, half(h)], mic[h][:, 0:HALF], ALU.subtract)
         for h in range(2):
-            nc.scalar.activation(e2[:, cols(h, 8, 8)], ne[:, cols(h)], ACT.Square)
+            nc.scalar.activation(err_sq[:, half(h, PAD)], neg_err[:, half(h)], ACT.Square)
+
+        rsqrt_pw = keep.tile([P, S], F32, name="rsqrt_pw")
         for h in range(2):
-            nc.scalar.activation(rp[:, cols(h)], pwt[h][:, 0:H], ACT.Abs_reciprocal_sqrt, bias=0.5)
-            for t in range(2):
-                nc.tensor.transpose(rpb[h][:, P * t : P * (t + 1)], rp[:, H * h + P * t : H * h + P * (t + 1)], ident[:])
+            nc.scalar.activation(rsqrt_pw[:, half(h)], power[:, half(h)], ACT.Abs_reciprocal_sqrt, bias=0.5)
+        sq_sum = keep.tile([P, S], F32, name="sq_sum")
         for h in range(2):
-            nc.vector.tensor_tensor(den[:, cols(h)], e2[:, cols(h, 7, 7)], m2[:, cols(h)], ALU.add)
+            nc.vector.tensor_tensor(sq_sum[:, half(h)], err_sq[:, half(h, PAD - 1)], mic_sq[:, half(h)], ALU.add)
+        rsqrt_den = keep.tile([P, S], F32, name="rsqrt_den")
         for h in range(2):
-            nc.scalar.activation(rd[:, cols(h)], den[:, cols(h)], ACT.Abs_reciprocal_sqrt, bias=0.4, scale=0.5)
-        warm2 = keep.tile([P, 8], F32, name="warm2")
-        nc.scalar.activation(warm2[:], rd[:, S - 8 : S], ACT.Tanh)
+            nc.scalar.activation(
+                rsqrt_den[:, half(h)], sq_sum[:, half(h)], ACT.Abs_reciprocal_sqrt, bias=0.4, scale=0.5
+            )
+        nc.scalar.activation(power[:, S - PAD : S], rsqrt_den[:, S - PAD : S], ACT.Tanh)
+
+        neg_st = keep.tile([P, S], F32, name="neg_st")
+        ratio = keep.tile([P, S], F32, name="ratio")
         for h in range(2):
-            nc.vector.tensor_tensor(u[:, cols(h)], ne[:, cols(h)], rpb[h][:, 0:H], ALU.mult)
+            nc.vector.tensor_tensor(neg_st[:, half(h)], neg_err[:, half(h)], rsqrt_pw[:, half(h)], ALU.mult)
         for h in range(2):
-            nc.vector.tensor_tensor(u[:, cols(h)], u[:, cols(h)], rpb[h][:, 0:H], ALU.mult)
+            nc.vector.tensor_tensor(neg_st[:, half(h)], neg_st[:, half(h)], rsqrt_pw[:, half(h)], ALU.mult)
         for h in range(2):
-            nc.vector.tensor_tensor(gg[:, cols(h)], e2[:, cols(h, 8, 8)], rd[:, cols(h)], ALU.mult)
+            nc.vector.tensor_tensor(ratio[:, half(h)], err_sq[:, half(h, PAD)], rsqrt_den[:, half(h)], ALU.mult)
         for h in range(2):
-            nc.vector.tensor_tensor(gg[:, cols(h)], gg[:, cols(h)], rd[:, cols(h)], ALU.mult)
-        for h in range(2):
-            nc.scalar.activation(den[:, cols(1 - h)], u[:, cols(h)], ACT.Tanh, scale=-2.0)
-            nc.vector.tensor_tensor(res[:, cols(h)], gg[:, cols(h)], den[:, cols(1 - h)], ALU.mult)
-            eng["sa"[h]].dma_start(out[:, cols(h)], res[:, cols(h)])
+            nc.vector.tensor_tensor(ratio[:, half(h)], ratio[:, half(h)], rsqrt_den[:, half(h)], ALU.mult)
+
+        result = keep.tile([P, S], F32, name="result")
+        for h, queue in enumerate((nc.sync, nc.scalar)):
+            bounded = sq_sum[:, half(1 - h)]
+            nc.scalar.activation(bounded, neg_st[:, half(h)], ACT.Tanh, scale=-2.0)
+            nc.vector.tensor_tensor(result[:, half(h)], ratio[:, half(h)], bounded, ALU.mult)
+            queue.dma_start(out[:, half(h)], result[:, half(h)])

@@ -28,7 +28,6 @@ AT_W1 = (WORDS_BYTES, WORDS_BYTES + 2 * RAW_BYTES)
 AT_X1 = 64
 AT_W2 = (AT_W1[0] + RAW_BYTES - 64, AT_W1[1])
 AT_X0 = 2 * WORDS_BYTES
-AT_ZERO = AT_X0 - PAD * 4
 AT_PAIRS = AT_X0 + WORDS_BYTES
 
 
@@ -48,14 +47,12 @@ def tile_picked_ynlms_dtd_p_kernel(
         offsets = keep.tile([P, S // 16], U16, name="offsets")
         nc.sync.dma_start(offsets[:], offs)
 
-        zero = shared.tile([P, 2 * PAD], F32, name="zero", offset=AT_ZERO)
-        nc.vector.memset(zero[:], 0.0)
         scale_rows = keep.tile([P, T], U8, name="scale_rows", align_bytes=64)
         nc.vector.memset(scale_rows[:].bitcast(I32), 0)
         far_sq = keep.tile([P, PAD + S], F32, name="far_sq")
         err_sq = keep.tile([P, PAD + S], F32, name="err_sq")
-        nc.vector.tensor_copy(far_sq[:, 0:PAD], zero[:, 0:PAD])
-        nc.vector.tensor_copy(err_sq[:, 0:PAD], zero[:, PAD : 2 * PAD])
+        nc.vector.memset(far_sq[:, 0:PAD], 0.0)
+        nc.vector.memset(err_sq[:, 0:PAD], 0.0)
         echo = keep.tile([P, S], F32, name="echo")
         nc.vector.memset(echo[:, 0:3], 0.0)
         ones = keep.tile([P, PAD], F32, name="ones")
@@ -93,11 +90,10 @@ def tile_picked_ynlms_dtd_p_kernel(
 
         raw_w1 = [load_weights(w1, g, "raw_w1_%d" % g, AT_W1[g]) for g in range(2)]
         words0 = load_words(0, AT_X0)
-        for r in range(4):
-            for g in range(2):
-                nc.scalar.dma_start(
-                    scale_rows[4 * g + r : P : 32, :].bitcast(I32), x_scales[g, r:16:4, :].bitcast(I32)
-                )
+        for q in range(4):
+            nc.scalar.dma_start(
+                scale_rows[32 * q : 32 * q + 8, :].bitcast(I32), x_scales[:, 4 * q : 4 * q + 4, :].bitcast(I32)
+            )
         preload_rsqrt = keep.tile([P, PAD], F32, name="preload_rsqrt")
         nc.scalar.activation(preload_rsqrt[:], ones[:], ACT.Abs_reciprocal_sqrt)
 

from contextlib import ExitStack

import concourse.mybir as mybir

K, T, S, N = 1024, 2048, 512, 128
FLOPS = 2 * 2 * K * N * S

F32 = mybir.dt.float32
BF16 = mybir.dt.bfloat16
U32 = mybir.dt.uint32
I32 = mybir.dt.int32
U16 = mybir.dt.uint16
U8 = mybir.dt.uint8
FP8X4 = mybir.dt.float8_e4m3fn_x4
ALU = mybir.AluOpType
ACT = mybir.ActivationFunctionType

P = 128
PACK = 4
K_PASS = P * PACK
HALF = S // 2
BANK = 512
PAD = 8

WORDS_BYTES = T * 4
RAW_BYTES = PACK * N * 4
AT_W1 = (WORDS_BYTES, WORDS_BYTES + 2 * RAW_BYTES)
AT_X1 = 64
AT_W2 = (AT_W1[0] + RAW_BYTES - 64, AT_W1[1])
AT_X0 = 2 * WORDS_BYTES
AT_PAIRS = AT_X0 + WORDS_BYTES


def tile_picked_ynlms_dtd_p_kernel(
    tc, x_words, x_scales, w1, w2, tap0, tap1, tap2, tap3, offs, out
):
    nc = tc.nc

    def half(h, shift=0):
        return slice(HALF * h + shift, HALF * (h + 1) + shift)

    with ExitStack() as ctx:
        keep = ctx.enter_context(tc.tile_pool(name="keep", bufs=1))
        shared = ctx.enter_context(tc.tile_pool(name="shared", bufs=1))
        psum = ctx.enter_context(tc.psum_pool(name="psum", bufs=1))

        offsets = keep.tile([P, S // 16], U16, name="offsets")
        nc.sync.dma_start(offsets[:], offs)

        scale_rows = keep.tile([P, T], U8, name="scale_rows", align_bytes=64)
        nc.vector.memset(scale_rows[:].bitcast(I32), 0)
        far_sq = keep.tile([P, PAD + S], F32, name="far_sq")
        err_sq = keep.tile([P, PAD + S], F32, name="err_sq")
        nc.vector.memset(far_sq[:, 0:PAD], 0.0)
        nc.vector.memset(err_sq[:, 0:PAD], 0.0)
        echo = keep.tile([P, S], F32, name="echo")
        nc.vector.memset(echo[:, 0:3], 0.0)
        ones = keep.tile([P, PAD], F32, name="ones")
        nc.vector.memset(ones[:], 1.0)

        taps = {}
        for s, tap in ((3, tap3), (2, tap2), (1, tap1), (0, tap0)):
            taps[s] = keep.tile([P, 1], F32, name="tap%d" % s)
            nc.gpsimd.dma_start(taps[s][:], tap)

        def load_weights(w, g, name, at):
            raw = shared.tile([P, PACK, N], F32, name=name, offset=at)
            nc.sync.dma_start(raw[:], w[K_PASS * g : K_PASS * (g + 1), :].rearrange("(p t) m -> p t m", t=PACK))
            return raw

        def load_words(g, at):
            words = shared.tile([P, T], U32, name="words%d" % g, offset=at)
            nc.sync.dma_start(words[:].bitcast(I32), x_words[g].rearrange("p n t -> p (n t)").bitcast(I32))
            return words

        def quantise(raw, name, copy, grouped):
            copy(
                grouped[:].rearrange("p (c i) t -> p c t i", i=4),
                raw[:].rearrange("p t (c i) -> p c t i", i=4),
            )
            codes = keep.tile([P, N], U32, name="codes_" + name, align_bytes=64)
            scales = keep.tile([P, N], U8, name="scales_" + name, align_bytes=64)
            nc.vector.quantize_mx(
                out=codes[:].bitcast(FP8X4), scales=scales[:], in_=grouped[:].rearrange("p m t -> p (m t)")
            )
            return codes, scales

        def grouped_tile(name):
            return keep.tile([P, N, PACK], BF16, name="grouped_" + name, align_bytes=64)

        raw_w1 = [load_weights(w1, g, "raw_w1_%d" % g, AT_W1[g]) for g in range(2)]
        words0 = load_words(0, AT_X0)
        for q in range(4):
            nc.scalar.dma_start(
                scale_rows[32 * q : 32 * q + 8, :].bitcast(I32), x_scales[:, 4 * q : 4 * q + 4, :].bitcast(I32)
            )
        preload_rsqrt = keep.tile([P, PAD], F32, name="preload_rsqrt")
        nc.scalar.activation(preload_rsqrt[:], ones[:], ACT.Abs_reciprocal_sqrt)

        q_w1 = [
            quantise(raw_w1[g], "w1_%d" % g, nc.vector.tensor_copy, grouped_tile("w1_%d" % g)) for g in range(2)
        ]
        words1 = load_words(1, AT_X1)
        raw_w2 = [load_weights(w2, g, "raw_w2_%d" % g, AT_W2[g]) for g in range(2)]

        picked_scales = keep.tile([P, S], U8, name="picked_scales", align_bytes=64)
        nc.vector.tensor_copy(picked_scales[:], scale_rows[:].indirect(offsets[:]))
        picked0 = keep.tile([P, S], U32, name="picked0", align_bytes=64)
        nc.vector.tensor_copy(picked0[:], words0[:].indirect(offsets[:]))

        far = [psum.tile([P, BANK], F32, name="far%d" % h) for h in range(2)]
        mic = [psum.tile([P, BANK], F32, name="mic%d" % h) for h in range(2)]

        def product_pass(bank, weights, g, h, picked):
            codes, scales = weights
            nc.tensor.matmul_mx(
                out=bank[:, 0:HALF],
                lhsT=codes[:].bitcast(FP8X4),
                lhsT_scale=scales[:],
                rhs=picked.bitcast(FP8X4),
                rhs_scale=picked_scales[4 * g : P, half(h)],
                start=(g == 0),
                stop=(g == 1),
            )

        for h in range(2):
            product_pass(far[h], q_w1[0], 0, h, picked0[:, half(h)])
        picked1 = []
        for h in range(2):
            picked1.append(keep.tile([P, HALF], U32, name="picked1_%d" % h, align_bytes=64))
            nc.vector.tensor_copy(picked1[h][:], words1[:].indirect(offsets[:, 16 * h : 16 * (h + 1)]))
            product_pass(far[h], q_w1[1], 1, h, picked1[h][:])
        last_grouped = shared.tile([P, N, PACK], BF16, name="grouped_w2_1", offset=AT_PAIRS, align_bytes=64)
        q_w2 = [
            quantise(raw_w2[0], "w2_0", nc.scalar.copy, grouped_tile("w2_0")),
            quantise(raw_w2[1], "w2_1", nc.vector.tensor_copy, last_grouped),
        ]
        for h in range(2):
            product_pass(mic[h], q_w2[0], 0, h, picked0[:, half(h)])
        for h in range(2):
            product_pass(mic[h], q_w2[1], 1, h, picked1[h][:])

        for h in range(2):
            n = HALF - 3 * h
            nc.scalar.activation(far_sq[:, half(h, PAD)], far[h][:, 0:HALF], ACT.Square)
            nc.scalar.activation(
                echo[:, HALF * h + 3 : HALF * h + 3 + n], far[h][:, 0:n], ACT.Copy, scale=taps[3][:]
            )

        pairs = shared.tile([P, PAD + S], F32, name="pairs", offset=AT_PAIRS)
        power = keep.tile([P, S], F32, name="power")
        for h in range(2):
            lo = HALF * h + PAD - (2 if h == 0 else 0)
            hi = HALF * (h + 1) + PAD
            nc.gpsimd.tensor_tensor(pairs[:, lo:hi], far_sq[:, lo:hi], far_sq[:, lo - 1 : hi - 1], ALU.add)
            nc.gpsimd.tensor_tensor(power[:, half(h)], pairs[:, half(h, PAD)], pairs[:, half(h, PAD - 2)], ALU.add)

        for s in (2, 1, 0):
            for h in range(2):
                n = HALF - s * h
                target = echo[:, HALF * h + s : HALF * h + s + n]
                nc.vector.scalar_tensor_tensor(target, far[h][:, 0:n], taps[s][:], target, ALU.mult, ALU.add)

        mic_sq = keep.tile([P, S], F32, name="mic_sq")
        neg_err = keep.tile([P, S], F32, name="neg_err")
        for h in range(2):
            nc.scalar.activation(mic_sq[:, half(h)], mic[h][:, 0:HALF], ACT.Square)
            nc.vector.tensor_tensor(neg_err[:, half(h)], echo[:, half(h)], mic[h][:, 0:HALF], ALU.subtract)
        for h in range(2):
            nc.scalar.activation(err_sq[:, half(h, PAD)], neg_err[:, half(h)], ACT.Square)

        rsqrt_pw = keep.tile([P, S], F32, name="rsqrt_pw")
        for h in range(2):
            nc.scalar.activation(rsqrt_pw[:, half(h)], power[:, half(h)], ACT.Abs_reciprocal_sqrt, bias=0.5)
        sq_sum = keep.tile([P, S], F32, name="sq_sum")
        for h in range(2):
            nc.vector.tensor_tensor(sq_sum[:, half(h)], err_sq[:, half(h, PAD - 1)], mic_sq[:, half(h)], ALU.add)
        rsqrt_den = keep.tile([P, S], F32, name="rsqrt_den")
        for h in range(2):
            nc.scalar.activation(
                rsqrt_den[:, half(h)], sq_sum[:, half(h)], ACT.Abs_reciprocal_sqrt, bias=0.4, scale=0.5
            )
        nc.scalar.activation(power[:, S - PAD : S], rsqrt_den[:, S - PAD : S], ACT.Tanh)

        neg_st = keep.tile([P, S], F32, name="neg_st")
        ratio = keep.tile([P, S], F32, name="ratio")
        for h in range(2):
            nc.vector.tensor_tensor(neg_st[:, half(h)], neg_err[:, half(h)], rsqrt_pw[:, half(h)], ALU.mult)
        for h in range(2):
            nc.vector.tensor_tensor(neg_st[:, half(h)], neg_st[:, half(h)], rsqrt_pw[:, half(h)], ALU.mult)
        for h in range(2):
            nc.vector.tensor_tensor(ratio[:, half(h)], err_sq[:, half(h, PAD)], rsqrt_den[:, half(h)], ALU.mult)
        for h in range(2):
            nc.vector.tensor_tensor(ratio[:, half(h)], ratio[:, half(h)], rsqrt_den[:, half(h)], ALU.mult)

        result = keep.tile([P, S], F32, name="result")
        for h, queue in enumerate((nc.sync, nc.scalar)):
            bounded = sq_sum[:, half(1 - h)]
            nc.scalar.activation(bounded, neg_st[:, half(h)], ACT.Tanh, scale=-2.0)
            nc.vector.tensor_tensor(result[:, half(h)], ratio[:, half(h)], bounded, ALU.mult)
            queue.dma_start(out[:, half(h)], result[:, half(h)])
